import numpy as np
CORES = [16,32,48,64,80]
N = 5
W = 64
def setup_inputs(rng):
    amp = 0.5 + 1.5 * rng.random((2, N, 128, 1), dtype=np.float32)
    return {"u": amp[0] * rng.standard_normal((N, 128, W), dtype=np.float32), "b": amp[1] * rng.standard_normal((N, 128, W), dtype=np.float32)}
def setup_inputs_big(rng):
    d = setup_inputs(rng)
    for k in ("u", "b"): d[k] = (d[k].astype(np.float32) * 1024.0).astype(d[k].dtype)
    return d
def setup_inputs_small(rng):
    d = setup_inputs(rng)
    for k in ("u", "b"): d[k] = (d[k].astype(np.float32) * (1 / 1024.0)).astype(d[k].dtype)
    return d
def setup_inputs_apart(rng):
    d = setup_inputs(rng)
    f = (10.0 ** rng.permutation(np.linspace(-1.5, 1.5, N))).astype(np.float32).reshape(N, 1, 1)
    for k in ("u", "b"): d[k] = (d[k].astype(np.float32) * f).astype(d[k].dtype)
    return d
def reference(u, b):
    g = np.concatenate(list(u.astype(np.float64)), axis=1); bb = np.concatenate(list(b.astype(np.float64)), axis=1)
    p = np.concatenate([g[:, -2:], g, g[:, :2]], axis=1)
    n = 0.125 * (p[:, :-4] + p[:, 1:-3] + p[:, 3:-1] + p[:, 4:]) + 0.5 * bb
    d = n - g
    s = np.stack([(d ** 2).mean(axis=1), np.abs(d).max(axis=1)], axis=1)
    return {"y": np.stack([n[:, W * r:W * r + W] for r in range(N)]).astype(np.float32), "s": np.broadcast_to(s.astype(np.float32), (N, 128, 2))}

@@ -1,0 +1,188 @@
+from concourse.bass import DstId, RemoteDMATransfer
+from concourse.mybir import AluOpType
+
+EARLY_HALO = False
+
+F32 = "float32"
+SCRATCH = {
+    "U0": ("sbuf", [128, 72], F32),
+    "Bb": ("sbuf", [128, 64], F32),
+    "cq": ("sbuf", [128, 68], F32),
+    "ch": ("sbuf", [128, 68], F32),
+    "P": ("sbuf", [128, 71], F32),
+    "Q": ("psum", [128, 68], F32),
+    "Wp": ("psum", [128, 68], F32),
+    "Np": ("psum", [128, 68], F32),
+    "ND": ("psum", [128, 60], F32),
+    "Big": ("sbuf", [128, 84], F32),
+    "DD": ("sbuf", [128, 60], F32),
+    "AD": ("sbuf", [128, 60], F32),
+    "T1": ("sbuf", [128, 64], F32),
+    "T2": ("sbuf", [128, 32], F32),
+    "F": ("sbuf", [128, 6, 24], F32),
+    "De": ("sbuf", [128, 5, 4], F32),
+    "Dn": ("sbuf", [128, 5, 4], F32),
+    "Z": ("sbuf", [128, 5, 4], F32),
+    "X1": ("sbuf", [128, 64], F32),
+    "X2": ("sbuf", [128, 32], F32),
+    "X3": ("sbuf", [128, 16], F32),
+    "X4": ("sbuf", [128, 8], F32),
+    "X5": ("sbuf", [128, 4], F32),
+    "res": ("sbuf", [128, 2], F32),
+    "cf": ("sbuf", [128, 2], F32),
+    "so": ("sbuf", [128, 2], F32),
+    "Ys": ("sbuf", [128, 64], F32),
+    "H": ("sbuf", [128, 4], F32),
+    "H8": ("sbuf", [128, 4], F32),
+    "c8": ("sbuf", [128, 4], F32),
+}
+SEMAPHORES = ["ldu", "ldb", "v", "pk", "arr", "halo", "sent", "yr", "sr", "sty", "sts"]
+
+
+def rank_program(g, core, T, topo):
+    rank = T.rank_of(core)
+    if rank is None:
+        return
+    n = len(T.cores)
+    ncol = n * 64
+    sem = T.sem
+    v = g.vector
+    add, sub, mul, mx = AluOpType.add, AluOpType.subtract, AluOpType.mult, AluOpType.max
+
+    last = [None]
+    cnt = {}
+
+    def dep():
+        if last[0] is not None:
+            v.wait_ge(last[0][0], last[0][1])
+
+    def done(ins, name):
+        cnt[name] = cnt.get(name, 0) + 1
+        ins.then_inc(sem[name], 1)
+        last[0] = (sem[name], cnt[name])
+
+    def tt(out, a, b, op, name="v"):
+        dep()
+        done(v.tensor_tensor(out, a, b, op), name)
+
+    def cp(out, a, name="v"):
+        dep()
+        done(v.tensor_copy(out, a), name)
+
+    def fill(ap, c):
+        dep()
+        done(v.memset(ap, c), "v")
+
+    def peer(j):
+        return T.cores[(rank + j) % n]
+
+    def dst_id(c):
+        rid, pid, _ = topo.addr(c)
+        return DstId(rid=rid, pnc=pid)
+
+    def engines(dsts):
+        m = topo.mask(core, dsts[0])
+        for c in dsts[1:]:
+            m &= topo.mask(core, c)
+        return [1 << i for i in range(16) if (m >> i) & 1]
+
+    U0, Bb, P, Q, Wp, Np, ND, Big, DD, AD = T.U0, T.Bb, T.P, T.Q, T.Wp, T.Np, T.ND, T.Big, T.DD, T.AD
+    T1, T2, F, De, Dn, Z = T.T1, T.T2, T.F, T.De, T.Dn, T.Z
+    X1, X2, X3, X4, X5 = T.X1, T.X2, T.X3, T.X4, T.X5
+
+    g.sync.dma_start(U0[:, 4:68], T.u[:, :]).then_inc(sem.ldu, 16)
+    g.scalar.dma_start(Bb[:, :], T.b[:, :]).then_inc(sem.ldb, 16)
+
+    fill(U0[:, 0:4], 0.0)
+    fill(U0[:, 68:72], 0.0)
+    fill(T.cq[:, :], 0.25)
+    fill(T.ch[:, :], 0.5)
+    fill(T1[:, :], 0.0)
+
+    sent = 0
+    if EARLY_HALO:
+        left, right = peer(-1), peer(1)
+        eng = engines([left, right])
+        half = len(eng) // 2
+        g.wait_ge(sem.ldu, 16)
+        g.remote_dma_fused([
+            RemoteDMATransfer(dst_ids=[dst_id(left)], dma_engine_mask=sum(eng[:half]), remote_sem=sem.halo,
+                              src=U0[:, 4:6], dst=T.H[:, 2:4]),
+            RemoteDMATransfer(dst_ids=[dst_id(right)], dma_engine_mask=sum(eng[half:]), remote_sem=sem.halo,
+                              src=U0[:, 66:68], dst=T.H[:, 0:2]),
+        ], local_sem=sem.sent)
+        sent += len(eng)
+
+    v.wait_ge(sem.ldu, 16)
+    tt(P[:, :], U0[:, 0:71], U0[:, 1:72], add)
+    tt(Q[:, :], P[:, 0:68], P[:, 3:71], add)
+    tt(Wp[:, :], Q[:, :], T.cq[:, :], mul)
+    v.wait_ge(sem.ldb, 16)
+    tt(Wp[:, 2:66], Wp[:, 2:66], Bb[:, :], add)
+    tt(Np[:, :], Wp[:, :], T.ch[:, :], mul)
+    tt(Big[:, 20:84], Np[:, 0:64], U0[:, 2:66], sub)
+    tt(ND[:, :], U0[:, 6:66], Np[:, 4:64], sub)
+    tt(Big[:, 0:4], Np[:, 64:68], U0[:, 66:70], sub)
+    tt(DD[:, :], Big[:, 24:84], ND[:, :], mul)
+    tt(AD[:, :], Big[:, 24:84], ND[:, :], mx)
+    tt(T1[:, 0:30], DD[:, 0:30], DD[:, 30:60], add)
+    tt(T1[:, 32:62], AD[:, 0:30], AD[:, 30:60], mx)
+    tt(T2[:, 0:16], T1[:, 0:16], T1[:, 16:32], add)
+    tt(T2[:, 16:32], T1[:, 32:48], T1[:, 48:64], mx)
+    tt(Big[:, 12:20], T2[:, 0:8], T2[:, 8:16], add)
+    tt(Big[:, 4:12], T2[:, 16:24], T2[:, 24:32], mx, "pk")
+
+    others = [peer(j) for j in range(1, n)]
+    eng = engines(others)
+    g.wait_ge(sem.pk, 1)
+    g.remote_dma_fused([
+        RemoteDMATransfer(dst_ids=[dst_id(c) for c in others], dma_engine_mask=sum(eng), remote_sem=sem.arr,
+                          srcs=[Big[:, 0:24]], dsts=[F[:, n - j, :] for j in range(1, n)]),
+    ], local_sem=sem.sent)
+    sent += len(eng)
+
+    cp(F[:, 0, :], Big[:, 0:24])
+    cp(F[:, n, 20:24], Big[:, 20:24])
+    cp(T.Ys[:, :], Np[:, 2:66])
+    fill(X1[:, :], 0.0)
+    fill(Z[:, :, :], 0.0)
+    fill(T.cf[:, 0:1], -1.0 / ncol)
+    fill(T.cf[:, 1:2], 1.0)
+    if EARLY_HALO:
+        fill(T.c8[:, :], 0.125)
+        v.wait_ge(sem.halo, len(eng))
+        tt(T.H8[:, :], T.H[:, :], T.c8[:, :], mul)
+        tt(T.Ys[:, 0:2], T.Ys[:, 0:2], T.H8[:, 0:2], add)
+        tt(T.Ys[:, 0:1], T.Ys[:, 0:1], T.H8[:, 1:2], add)
+        tt(T.Ys[:, 62:64], T.Ys[:, 62:64], T.H8[:, 2:4], add)
+        tt(T.Ys[:, 63:64], T.Ys[:, 63:64], T.H8[:, 2:3], add, "yr")
+
+    v.wait_ge(sem.arr, (n - 1) * len(eng))
+    tt(De[:, :, :], F[:, 0:n, 0:4], F[:, 1:n + 1, 20:24], add)
+    if not EARLY_HALO:
+        tt(T.Ys[:, 62:64], De[:, 0, 0:2], U0[:, 66:68], add)
+        tt(T.Ys[:, 0:2], De[:, n - 1, 2:4], U0[:, 4:6], add, "yr")
+    tt(Dn[:, :, :], Z[:, :, :], De[:, :, :], sub)
+    tt(F[:, 0:n, 0:4], De[:, :, :], Dn[:, :, :], mx)
+    tt(F[:, 0:n, 20:24], De[:, :, :], Dn[:, :, :], mul)
+    tt(X1[:, 0:30], F[:, 0:n, 12:18], F[:, 0:n, 18:24], add)
+    tt(X1[:, 32:62], F[:, 0:n, 0:6], F[:, 0:n, 6:12], mx)
+    tt(X2[:, 0:16], X1[:, 0:16], X1[:, 16:32], add)
+    tt(X2[:, 16:32], X1[:, 32:48], X1[:, 48:64], mx)
+    tt(X3[:, 0:8], X2[:, 0:8], X2[:, 8:16], add)
+    tt(X3[:, 8:16], X2[:, 16:24], X2[:, 24:32], mx)
+    tt(X4[:, 0:4], X3[:, 0:4], X3[:, 4:8], add)
+    tt(X4[:, 4:8], X3[:, 8:12], X3[:, 12:16], mx)
+    tt(X5[:, 0:2], X4[:, 0:2], X4[:, 2:4], add)
+    tt(X5[:, 2:4], X4[:, 4:6], X4[:, 6:8], mx)
+    tt(T.res[:, 0:1], X5[:, 0:1], X5[:, 1:2], add)
+    tt(T.res[:, 1:2], X5[:, 2:3], X5[:, 3:4], mx)
+    tt(T.so[:, :], T.res[:, :], T.cf[:, :], mul, "sr")
+
+    g.scalar.wait_ge(sem.yr, 1)
+    g.scalar.dma_start(T.y[:, :], T.Ys[:, :]).then_inc(sem.sty, 16)
+    g.scalar.wait_ge(sem.sty, 16)
+    g.sync.wait_ge(sem.sr, 1)
+    g.sync.dma_start(T.s[:, :], T.so[:, :]).then_inc(sem.sts, 16)
+    g.sync.wait_ge(sem.sts, 16)
+    g.wait_ge(sem.sent, sent)

@@ -1,18 +1,18 @@
 from concourse.bass import DstId, RemoteDMATransfer
 from concourse.mybir import AluOpType
 
-EARLY_HALO = False
-
 F32 = "float32"
 SCRATCH = {
     "U0": ("sbuf", [128, 72], F32),
-    "Bb": ("sbuf", [128, 64], F32),
-    "cq": ("sbuf", [128, 68], F32),
-    "ch": ("sbuf", [128, 68], F32),
+    "Bb": ("sbuf", [128, 72], F32),
+    "chp": ("psum", [128, 68], F32),
+    "c8": ("sbuf", [128, 68], F32),
     "P": ("sbuf", [128, 71], F32),
     "Q": ("psum", [128, 68], F32),
-    "Wp": ("psum", [128, 68], F32),
-    "Np": ("psum", [128, 68], F32),
+    "Q8": ("psum", [128, 68], F32),
+    "HB": ("psum", [128, 68], F32),
+    "Zs": ("sbuf", [128, 68], F32),
+    "NZ": ("sbuf", [128, 68], F32),
     "ND": ("psum", [128, 60], F32),
     "Big": ("sbuf", [128, 84], F32),
     "DD": ("sbuf", [128, 60], F32),
@@ -28,15 +28,12 @@ SCRATCH = {
     "X3": ("sbuf", [128, 16], F32),
     "X4": ("sbuf", [128, 8], F32),
     "X5": ("sbuf", [128, 4], F32),
-    "res": ("sbuf", [128, 2], F32),
-    "cf": ("sbuf", [128, 2], F32),
+    "rs": ("sbuf", [128, 1], F32),
+    "cf": ("sbuf", [128, 1], F32),
     "so": ("sbuf", [128, 2], F32),
     "Ys": ("sbuf", [128, 64], F32),
-    "H": ("sbuf", [128, 4], F32),
-    "H8": ("sbuf", [128, 4], F32),
-    "c8": ("sbuf", [128, 4], F32),
 }
-SEMAPHORES = ["ldu", "ldb", "v", "pk", "arr", "halo", "sent", "yr", "sr", "sty", "sts"]
+SEMAPHORES = ["ldu", "ldb", "va", "vb", "vc", "arr", "sent", "yr", "sr", "sty", "sts"]
 
 
 def rank_program(g, core, T, topo):
@@ -49,29 +46,27 @@ def rank_program(g, core, T, topo):
     v = g.vector
     add, sub, mul, mx = AluOpType.add, AluOpType.subtract, AluOpType.mult, AluOpType.max
 
-    last = [None]
-    cnt = {}
+    cnt = {"va": 0, "vb": 0, "vc": 0, "yr": 0, "sr": 0}
 
-    def dep():
-        if last[0] is not None:
-            v.wait_ge(last[0][0], last[0][1])
+    def wait(w):
+        for c in w:
+            if cnt[c]:
+                v.wait_ge(sem[c], cnt[c])
 
-    def done(ins, name):
-        cnt[name] = cnt.get(name, 0) + 1
-        ins.then_inc(sem[name], 1)
-        last[0] = (sem[name], cnt[name])
+    def done(ins, ch):
+        cnt[ch] += 1
+        ins.then_inc(sem[ch], 1)
 
-    def tt(out, a, b, op, name="v"):
-        dep()
-        done(v.tensor_tensor(out, a, b, op), name)
+    def tt(out, a, b, op, ch, w=()):
+        wait(w)
+        done(v.tensor_tensor(out, a, b, op), ch)
 
-    def cp(out, a, name="v"):
-        dep()
-        done(v.tensor_copy(out, a), name)
+    def cp(out, a, w=()):
+        wait(w)
+        done(v.tensor_copy(out, a), "va")
 
     def fill(ap, c):
-        dep()
-        done(v.memset(ap, c), "v")
+        done(v.memset(ap, c), "va")
 
     def peer(j):
         return T.cores[(rank + j) % n]
@@ -86,103 +81,84 @@ def rank_program(g, core, T, topo):
             m &= topo.mask(core, c)
         return [1 << i for i in range(16) if (m >> i) & 1]
 
-    U0, Bb, P, Q, Wp, Np, ND, Big, DD, AD = T.U0, T.Bb, T.P, T.Q, T.Wp, T.Np, T.ND, T.Big, T.DD, T.AD
+    U0, Bb, P, Q, Q8, HB, Zs, NZ, ND, Big, DD, AD = (T.U0, T.Bb, T.P, T.Q, T.Q8, T.HB, T.Zs, T.NZ, T.ND, T.Big, T.DD,
+                                                     T.AD)
     T1, T2, F, De, Dn, Z = T.T1, T.T2, T.F, T.De, T.Dn, T.Z
     X1, X2, X3, X4, X5 = T.X1, T.X2, T.X3, T.X4, T.X5
+    A_, B_, C_ = ("va",), ("vb",), ("vc",)
 
     g.sync.dma_start(U0[:, 4:68], T.u[:, :]).then_inc(sem.ldu, 16)
-    g.scalar.dma_start(Bb[:, :], T.b[:, :]).then_inc(sem.ldb, 16)
+    g.scalar.dma_start(Bb[:, 4:68], T.b[:, :]).then_inc(sem.ldb, 16)
 
     fill(U0[:, 0:4], 0.0)
     fill(U0[:, 68:72], 0.0)
-    fill(T.cq[:, :], 0.25)
-    fill(T.ch[:, :], 0.5)
+    fill(Bb[:, 0:4], 0.0)
+    fill(Bb[:, 68:72], 0.0)
+    fill(T.chp[:, :], 0.5)
+    fill(T.c8[:, :], 0.125)
     fill(T1[:, :], 0.0)
 
-    sent = 0
-    if EARLY_HALO:
-        left, right = peer(-1), peer(1)
-        eng = engines([left, right])
-        half = len(eng) // 2
-        g.wait_ge(sem.ldu, 16)
-        g.remote_dma_fused([
-            RemoteDMATransfer(dst_ids=[dst_id(left)], dma_engine_mask=sum(eng[:half]), remote_sem=sem.halo,
-                              src=U0[:, 4:6], dst=T.H[:, 2:4]),
-            RemoteDMATransfer(dst_ids=[dst_id(right)], dma_engine_mask=sum(eng[half:]), remote_sem=sem.halo,
-                              src=U0[:, 66:68], dst=T.H[:, 0:2]),
-        ], local_sem=sem.sent)
-        sent += len(eng)
-
     v.wait_ge(sem.ldu, 16)
-    tt(P[:, :], U0[:, 0:71], U0[:, 1:72], add)
-    tt(Q[:, :], P[:, 0:68], P[:, 3:71], add)
-    tt(Wp[:, :], Q[:, :], T.cq[:, :], mul)
+    tt(P[:, :], U0[:, 0:71], U0[:, 1:72], add, "va", A_)
     v.wait_ge(sem.ldb, 16)
-    tt(Wp[:, 2:66], Wp[:, 2:66], Bb[:, :], add)
-    tt(Np[:, :], Wp[:, :], T.ch[:, :], mul)
-    tt(Big[:, 20:84], Np[:, 0:64], U0[:, 2:66], sub)
-    tt(ND[:, :], U0[:, 6:66], Np[:, 4:64], sub)
-    tt(Big[:, 0:4], Np[:, 64:68], U0[:, 66:70], sub)
-    tt(DD[:, :], Big[:, 24:84], ND[:, :], mul)
-    tt(AD[:, :], Big[:, 24:84], ND[:, :], mx)
-    tt(T1[:, 0:30], DD[:, 0:30], DD[:, 30:60], add)
-    tt(T1[:, 32:62], AD[:, 0:30], AD[:, 30:60], mx)
-    tt(T2[:, 0:16], T1[:, 0:16], T1[:, 16:32], add)
-    tt(T2[:, 16:32], T1[:, 32:48], T1[:, 48:64], mx)
-    tt(Big[:, 12:20], T2[:, 0:8], T2[:, 8:16], add)
-    tt(Big[:, 4:12], T2[:, 16:24], T2[:, 24:32], mx, "pk")
+    tt(HB[:, :], Bb[:, 2:70], T.chp[:, :], mul, "vc")
+    tt(Q[:, :], P[:, 0:68], P[:, 3:71], add, "va", A_)
+    tt(Zs[:, :], HB[:, :], U0[:, 2:70], sub, "vb", C_)
+    tt(Q8[:, :], Q[:, :], T.c8[:, :], mul, "va", A_)
+    tt(NZ[:, :], U0[:, 2:70], HB[:, :], sub, "vc")
+    tt(Big[:, 20:84], Q8[:, 0:64], Zs[:, 0:64], add, "va", ("va", "vb"))
+    tt(ND[:, :], NZ[:, 4:64], Q8[:, 4:64], sub, "vc", C_)
+    tt(Big[:, 0:4], Q8[:, 64:68], Zs[:, 64:68], add, "vb")
+    tt(DD[:, :], Big[:, 24:84], ND[:, :], mul, "va", ("va", "vc"))
+    tt(AD[:, :], Big[:, 24:84], ND[:, :], mx, "vb")
+    tt(T1[:, 0:30], DD[:, 0:30], DD[:, 30:60], add, "va", A_)
+    tt(T1[:, 32:62], AD[:, 0:30], AD[:, 30:60], mx, "vb", B_)
+    tt(T2[:, 0:16], T1[:, 0:16], T1[:, 16:32], add, "va", A_)
+    tt(T2[:, 16:32], T1[:, 32:48], T1[:, 48:64], mx, "vb", B_)
+    tt(Big[:, 12:20], T2[:, 0:8], T2[:, 8:16], add, "va", A_)
+    tt(Big[:, 4:12], T2[:, 16:24], T2[:, 24:32], mx, "vb", B_)
 
     others = [peer(j) for j in range(1, n)]
     eng = engines(others)
-    g.wait_ge(sem.pk, 1)
+    g.wait_ge(sem.va, cnt["va"])
+    g.wait_ge(sem.vb, cnt["vb"])
     g.remote_dma_fused([
         RemoteDMATransfer(dst_ids=[dst_id(c) for c in others], dma_engine_mask=sum(eng), remote_sem=sem.arr,
                           srcs=[Big[:, 0:24]], dsts=[F[:, n - j, :] for j in range(1, n)]),
     ], local_sem=sem.sent)
-    sent += len(eng)
 
-    cp(F[:, 0, :], Big[:, 0:24])
+    cp(F[:, 0, :], Big[:, 0:24], ("va", "vb"))
     cp(F[:, n, 20:24], Big[:, 20:24])
-    cp(T.Ys[:, :], Np[:, 2:66])
+    tt(T.Ys[:, 2:62], Big[:, 24:84], U0[:, 6:66], add, "va")
     fill(X1[:, :], 0.0)
     fill(Z[:, :, :], 0.0)
-    fill(T.cf[:, 0:1], -1.0 / ncol)
-    fill(T.cf[:, 1:2], 1.0)
-    if EARLY_HALO:
-        fill(T.c8[:, :], 0.125)
-        v.wait_ge(sem.halo, len(eng))
-        tt(T.H8[:, :], T.H[:, :], T.c8[:, :], mul)
-        tt(T.Ys[:, 0:2], T.Ys[:, 0:2], T.H8[:, 0:2], add)
-        tt(T.Ys[:, 0:1], T.Ys[:, 0:1], T.H8[:, 1:2], add)
-        tt(T.Ys[:, 62:64], T.Ys[:, 62:64], T.H8[:, 2:4], add)
-        tt(T.Ys[:, 63:64], T.Ys[:, 63:64], T.H8[:, 2:3], add, "yr")
+    fill(T.cf[:, :], -1.0 / ncol)
 
     v.wait_ge(sem.arr, (n - 1) * len(eng))
-    tt(De[:, :, :], F[:, 0:n, 0:4], F[:, 1:n + 1, 20:24], add)
-    if not EARLY_HALO:
-        tt(T.Ys[:, 62:64], De[:, 0, 0:2], U0[:, 66:68], add)
-        tt(T.Ys[:, 0:2], De[:, n - 1, 2:4], U0[:, 4:6], add, "yr")
-    tt(Dn[:, :, :], Z[:, :, :], De[:, :, :], sub)
-    tt(F[:, 0:n, 0:4], De[:, :, :], Dn[:, :, :], mx)
-    tt(F[:, 0:n, 20:24], De[:, :, :], Dn[:, :, :], mul)
-    tt(X1[:, 0:30], F[:, 0:n, 12:18], F[:, 0:n, 18:24], add)
-    tt(X1[:, 32:62], F[:, 0:n, 0:6], F[:, 0:n, 6:12], mx)
-    tt(X2[:, 0:16], X1[:, 0:16], X1[:, 16:32], add)
-    tt(X2[:, 16:32], X1[:, 32:48], X1[:, 48:64], mx)
-    tt(X3[:, 0:8], X2[:, 0:8], X2[:, 8:16], add)
-    tt(X3[:, 8:16], X2[:, 16:24], X2[:, 24:32], mx)
-    tt(X4[:, 0:4], X3[:, 0:4], X3[:, 4:8], add)
-    tt(X4[:, 4:8], X3[:, 8:12], X3[:, 12:16], mx)
-    tt(X5[:, 0:2], X4[:, 0:2], X4[:, 2:4], add)
-    tt(X5[:, 2:4], X4[:, 4:6], X4[:, 6:8], mx)
-    tt(T.res[:, 0:1], X5[:, 0:1], X5[:, 1:2], add)
-    tt(T.res[:, 1:2], X5[:, 2:3], X5[:, 3:4], mx)
-    tt(T.so[:, :], T.res[:, :], T.cf[:, :], mul, "sr")
+    tt(De[:, :, :], F[:, 0:n, 0:4], F[:, 1:n + 1, 20:24], add, "va", A_)
+    tt(Dn[:, :, :], Z[:, :, :], De[:, :, :], sub, "va", A_)
+    tt(T.Ys[:, 62:64], De[:, 0, 0:2], U0[:, 66:68], add, "yr")
+    tt(T.Ys[:, 0:2], De[:, n - 1, 2:4], U0[:, 4:6], add, "yr")
+    tt(F[:, 0:n, 20:24], De[:, :, :], Dn[:, :, :], mul, "va", A_)
+    tt(F[:, 0:n, 0:4], De[:, :, :], Dn[:, :, :], mx, "vb")
+    tt(X1[:, 0:30], F[:, 0:n, 12:18], F[:, 0:n, 18:24], add, "va", A_)
+    tt(X1[:, 32:62], F[:, 0:n, 0:6], F[:, 0:n, 6:12], mx, "vb", B_)
+    tt(X2[:, 0:16], X1[:, 0:16], X1[:, 16:32], add, "va", A_)
+    tt(X2[:, 16:32], X1[:, 32:48], X1[:, 48:64], mx, "vb", B_)
+    tt(X3[:, 0:8], X2[:, 0:8], X2[:, 8:16], add, "va", A_)
+    tt(X3[:, 8:16], X2[:, 16:24], X2[:, 24:32], mx, "vb", B_)
+    tt(X4[:, 0:4], X3[:, 0:4], X3[:, 4:8], add, "va", A_)
+    tt(X4[:, 4:8], X3[:, 8:12], X3[:, 12:16], mx, "vb", B_)
+    tt(X5[:, 0:2], X4[:, 0:2], X4[:, 2:4], add, "va", A_)
+    tt(X5[:, 2:4], X4[:, 4:6], X4[:, 6:8], mx, "vb", B_)
+    tt(T.rs[:, :], X5[:, 0:1], X5[:, 1:2], add, "va", A_)
+    tt(T.so[:, 1:2], X5[:, 2:3], X5[:, 3:4], mx, "sr", B_)
+    tt(T.so[:, 0:1], T.rs[:, :], T.cf[:, :], mul, "sr", A_)
 
-    g.scalar.wait_ge(sem.yr, 1)
+    g.scalar.wait_ge(sem.yr, 2)
     g.scalar.dma_start(T.y[:, :], T.Ys[:, :]).then_inc(sem.sty, 16)
     g.scalar.wait_ge(sem.sty, 16)
-    g.sync.wait_ge(sem.sr, 1)
+    g.sync.wait_ge(sem.sr, 2)
     g.sync.dma_start(T.s[:, :], T.so[:, :]).then_inc(sem.sts, 16)
     g.sync.wait_ge(sem.sts, 16)
-    g.wait_ge(sem.sent, sent)
+    g.wait_ge(sem.sent, len(eng))

@@ -23,6 +23,10 @@ SCRATCH = {
     "De": ("sbuf", [128, 5, 4], F32),
     "Dn": ("sbuf", [128, 5, 4], F32),
     "Z": ("sbuf", [128, 5, 4], F32),
+    "Sa": ("sbuf", [128, 20], F32),
+    "Ma": ("sbuf", [128, 20], F32),
+    "SQ": ("sbuf", [128, 20], F32),
+    "AE": ("sbuf", [128, 20], F32),
     "X1": ("sbuf", [128, 64], F32),
     "X2": ("sbuf", [128, 32], F32),
     "X3": ("sbuf", [128, 16], F32),
@@ -32,8 +36,10 @@ SCRATCH = {
     "cf": ("sbuf", [128, 1], F32),
     "so": ("sbuf", [128, 2], F32),
     "Ys": ("sbuf", [128, 64], F32),
+    "H": ("sbuf", [128, 4], F32),
+    "H8": ("sbuf", [128, 4], F32),
 }
-SEMAPHORES = ["ldu", "ldb", "va", "vb", "vc", "arr", "sent", "yr", "sr", "sty", "sts"]
+SEMAPHORES = ["ldu", "ldb", "va", "vb", "vc", "arr", "halo", "sent", "yr", "sr", "sty", "sts"]
 
 
 def rank_program(g, core, T, topo):
@@ -83,7 +89,7 @@ def rank_program(g, core, T, topo):
 
     U0, Bb, P, Q, Q8, HB, Zs, NZ, ND, Big, DD, AD = (T.U0, T.Bb, T.P, T.Q, T.Q8, T.HB, T.Zs, T.NZ, T.ND, T.Big, T.DD,
                                                      T.AD)
-    T1, T2, F, De, Dn, Z = T.T1, T.T2, T.F, T.De, T.Dn, T.Z
+    T1, T2, F, De, Dn, Z, Ys, H8 = T.T1, T.T2, T.F, T.De, T.Dn, T.Z, T.Ys, T.H8
     X1, X2, X3, X4, X5 = T.X1, T.X2, T.X3, T.X4, T.X5
     A_, B_, C_ = ("va",), ("vb",), ("vc",)
 
@@ -97,6 +103,17 @@ def rank_program(g, core, T, topo):
     fill(T.chp[:, :], 0.5)
     fill(T.c8[:, :], 0.125)
     fill(T1[:, :], 0.0)
+
+    left, right = peer(-1), peer(1)
+    heng = engines([left, right])
+    half = len(heng) // 2
+    g.wait_ge(sem.ldu, 16)
+    g.remote_dma_fused([
+        RemoteDMATransfer(dst_ids=[dst_id(left)], dma_engine_mask=sum(heng[:half]), remote_sem=sem.halo,
+                          src=U0[:, 4:6], dst=T.H[:, 2:4]),
+        RemoteDMATransfer(dst_ids=[dst_id(right)], dma_engine_mask=sum(heng[half:]), remote_sem=sem.halo,
+                          src=U0[:, 66:68], dst=T.H[:, 0:2]),
+    ], local_sem=sem.sent)
 
     v.wait_ge(sem.ldu, 16)
     tt(P[:, :], U0[:, 0:71], U0[:, 1:72], add, "va", A_)
@@ -129,20 +146,27 @@ def rank_program(g, core, T, topo):
 
     cp(F[:, 0, :], Big[:, 0:24], ("va", "vb"))
     cp(F[:, n, 20:24], Big[:, 20:24])
-    tt(T.Ys[:, 2:62], Big[:, 24:84], U0[:, 6:66], add, "va")
+    tt(Ys[:, 0:62], Big[:, 22:84], U0[:, 4:66], add, "va")
+    tt(Ys[:, 62:64], Big[:, 0:2], U0[:, 66:68], add, "va")
     fill(X1[:, :], 0.0)
     fill(Z[:, :, :], 0.0)
     fill(T.cf[:, :], -1.0 / ncol)
+    v.wait_ge(sem.halo, len(heng))
+    tt(H8[:, :], T.H[:, :], T.c8[:, 0:4], mul, "vc")
+    tt(Ys[:, 0:2], Ys[:, 0:2], H8[:, 0:2], add, "vc", ("va", "vc"))
+    tt(Ys[:, 62:64], Ys[:, 62:64], H8[:, 2:4], add, "vb")
+    tt(Ys[:, 0:1], Ys[:, 0:1], H8[:, 1:2], add, "yr", C_)
+    tt(Ys[:, 63:64], Ys[:, 63:64], H8[:, 2:3], add, "yr", B_)
 
     v.wait_ge(sem.arr, (n - 1) * len(eng))
-    tt(De[:, :, :], F[:, 0:n, 0:4], F[:, 1:n + 1, 20:24], add, "va", A_)
+    tt(De[:, :, :], F[:, 0:n, 0:4], F[:, 1:n + 1, 20:24], add, "va")
+    tt(T.Sa[:, :], F[:, 0:n, 12:16], F[:, 0:n, 16:20], add, "vc")
     tt(Dn[:, :, :], Z[:, :, :], De[:, :, :], sub, "va", A_)
-    tt(T.Ys[:, 62:64], De[:, 0, 0:2], U0[:, 66:68], add, "yr")
-    tt(T.Ys[:, 0:2], De[:, n - 1, 2:4], U0[:, 4:6], add, "yr")
-    tt(F[:, 0:n, 20:24], De[:, :, :], Dn[:, :, :], mul, "va", A_)
-    tt(F[:, 0:n, 0:4], De[:, :, :], Dn[:, :, :], mx, "vb")
-    tt(X1[:, 0:30], F[:, 0:n, 12:18], F[:, 0:n, 18:24], add, "va", A_)
-    tt(X1[:, 32:62], F[:, 0:n, 0:6], F[:, 0:n, 6:12], mx, "vb", B_)
+    tt(T.Ma[:, :], F[:, 0:n, 4:8], F[:, 0:n, 8:12], mx, "vc")
+    tt(T.SQ[:, :], De[:, :, :], Dn[:, :, :], mul, "va", A_)
+    tt(T.AE[:, :], De[:, :, :], Dn[:, :, :], mx, "vb")
+    tt(X1[:, 0:20], T.SQ[:, :], T.Sa[:, :], add, "va", ("va", "vc"))
+    tt(X1[:, 32:52], T.AE[:, :], T.Ma[:, :], mx, "vb", B_)
     tt(X2[:, 0:16], X1[:, 0:16], X1[:, 16:32], add, "va", A_)
     tt(X2[:, 16:32], X1[:, 32:48], X1[:, 48:64], mx, "vb", B_)
     tt(X3[:, 0:8], X2[:, 0:8], X2[:, 8:16], add, "va", A_)
@@ -156,9 +180,9 @@ def rank_program(g, core, T, topo):
     tt(T.so[:, 0:1], T.rs[:, :], T.cf[:, :], mul, "sr", A_)
 
     g.scalar.wait_ge(sem.yr, 2)
-    g.scalar.dma_start(T.y[:, :], T.Ys[:, :]).then_inc(sem.sty, 16)
+    g.scalar.dma_start(T.y[:, :], Ys[:, :]).then_inc(sem.sty, 16)
     g.scalar.wait_ge(sem.sty, 16)
     g.sync.wait_ge(sem.sr, 2)
     g.sync.dma_start(T.s[:, :], T.so[:, :]).then_inc(sem.sts, 16)
     g.sync.wait_ge(sem.sts, 16)
-    g.wait_ge(sem.sent, len(eng))
+    g.wait_ge(sem.sent, len(eng) + len(heng))

@@ -1,45 +1,30 @@
+import math
 from concourse.bass import DstId, RemoteDMATransfer
-from concourse.mybir import AluOpType
+from concourse.mybir import AluOpType, AxisListType, ActivationFunctionType
 
 F32 = "float32"
 SCRATCH = {
     "U0": ("sbuf", [128, 72], F32),
-    "Bb": ("sbuf", [128, 72], F32),
-    "chp": ("psum", [128, 68], F32),
-    "c8": ("sbuf", [128, 68], F32),
+    "Bb": ("sbuf", [128, 64], F32),
+    "U8": ("psum", [128, 512], F32),
+    "B4": ("sbuf", [128, 64], F32),
     "P": ("sbuf", [128, 71], F32),
-    "Q": ("psum", [128, 68], F32),
-    "Q8": ("psum", [128, 68], F32),
-    "HB": ("psum", [128, 68], F32),
-    "Zs": ("sbuf", [128, 68], F32),
-    "NZ": ("sbuf", [128, 68], F32),
-    "ND": ("psum", [128, 60], F32),
-    "Big": ("sbuf", [128, 84], F32),
-    "DD": ("sbuf", [128, 60], F32),
-    "AD": ("sbuf", [128, 60], F32),
-    "T1": ("sbuf", [128, 64], F32),
-    "T2": ("sbuf", [128, 32], F32),
-    "F": ("sbuf", [128, 6, 24], F32),
-    "De": ("sbuf", [128, 5, 4], F32),
-    "Dn": ("sbuf", [128, 5, 4], F32),
-    "Z": ("sbuf", [128, 5, 4], F32),
-    "Sa": ("sbuf", [128, 20], F32),
-    "Ma": ("sbuf", [128, 20], F32),
-    "SQ": ("sbuf", [128, 20], F32),
-    "AE": ("sbuf", [128, 20], F32),
-    "X1": ("sbuf", [128, 64], F32),
-    "X2": ("sbuf", [128, 32], F32),
-    "X3": ("sbuf", [128, 16], F32),
-    "X4": ("sbuf", [128, 8], F32),
-    "X5": ("sbuf", [128, 4], F32),
-    "rs": ("sbuf", [128, 1], F32),
-    "cf": ("sbuf", [128, 1], F32),
+    "Q": ("psum", [128, 512], F32),
+    "Z8": ("sbuf", [128, 68], F32),
+    "Big": ("sbuf", [128, 72], F32),
+    "J": ("sbuf", [128, 60], F32),
+    "F": ("sbuf", [128, 6, 12], F32),
+    "G": ("sbuf", [128, 25], F32),
+    "Hs": ("sbuf", [128, 25], F32),
+    "R": ("sbuf", [128, 1], F32),
     "so": ("sbuf", [128, 2], F32),
+    "Y8": ("sbuf", [128, 64], F32),
     "Ys": ("sbuf", [128, 64], F32),
     "H": ("sbuf", [128, 4], F32),
-    "H8": ("sbuf", [128, 4], F32),
+    "Hc": ("sbuf", [128, 2], F32),
 }
-SEMAPHORES = ["ldu", "ldb", "va", "vb", "vc", "arr", "halo", "sent", "yr", "sr", "sty", "sts"]
+NK = 40
+SEMAPHORES = ["ldu", "ldb", "arr", "halo", "sent", "sty", "sts"] + ["k%d" % i for i in range(NK)]
 
 
 def rank_program(g, core, T, topo):
@@ -47,32 +32,29 @@ def rank_program(g, core, T, topo):
     if rank is None:
         return
     n = len(T.cores)
-    ncol = n * 64
     sem = T.sem
-    v = g.vector
+    v, sc, sy = g.vector, g.scalar, g.sync
     add, sub, mul, mx = AluOpType.add, AluOpType.subtract, AluOpType.mult, AluOpType.max
+    X = AxisListType.X
+    Copy, Square = ActivationFunctionType.Copy, ActivationFunctionType.Square
+    kq = 1.0 / (8.0 * math.sqrt(n * 64.0))
 
-    cnt = {"va": 0, "vb": 0, "vc": 0, "yr": 0, "sr": 0}
+    used = [0]
+    waited = {}
 
-    def wait(w):
-        for c in w:
-            if cnt[c]:
-                v.wait_ge(sem[c], cnt[c])
+    def done(ins):
+        nm = "k%d" % used[0]
+        used[0] += 1
+        ins.then_inc(sem[nm], 1)
+        return nm
 
-    def done(ins, ch):
-        cnt[ch] += 1
-        ins.then_inc(sem[ch], 1)
+    def need(q, *names):
+        for nm in names:
+            q.wait_ge(sem[nm], 1)
+            waited[nm] = True
 
-    def tt(out, a, b, op, ch, w=()):
-        wait(w)
-        done(v.tensor_tensor(out, a, b, op), ch)
-
-    def cp(out, a, w=()):
-        wait(w)
-        done(v.tensor_copy(out, a), "va")
-
-    def fill(ap, c):
-        done(v.memset(ap, c), "va")
+    def tt(out, a, b, op):
+        return done(v.tensor_tensor(out, a, b, op))
 
     def peer(j):
         return T.cores[(rank + j) % n]
@@ -87,22 +69,17 @@ def rank_program(g, core, T, topo):
             m &= topo.mask(core, c)
         return [1 << i for i in range(16) if (m >> i) & 1]
 
-    U0, Bb, P, Q, Q8, HB, Zs, NZ, ND, Big, DD, AD = (T.U0, T.Bb, T.P, T.Q, T.Q8, T.HB, T.Zs, T.NZ, T.ND, T.Big, T.DD,
-                                                     T.AD)
-    T1, T2, F, De, Dn, Z, Ys, H8 = T.T1, T.T2, T.F, T.De, T.Dn, T.Z, T.Ys, T.H8
-    X1, X2, X3, X4, X5 = T.X1, T.X2, T.X3, T.X4, T.X5
-    A_, B_, C_ = ("va",), ("vb",), ("vc",)
+    U0, Bb, U8, B4, P, Q, Z8, Big, F, G, Hs, Y8, Ys, H, Hc = (T.U0, T.Bb, T.U8, T.B4, T.P, T.Q, T.Z8, T.Big, T.F, T.G,
+                                                              T.Hs, T.Y8, T.Ys, T.H, T.Hc)
 
-    g.sync.dma_start(U0[:, 4:68], T.u[:, :]).then_inc(sem.ldu, 16)
-    g.scalar.dma_start(Bb[:, 4:68], T.b[:, :]).then_inc(sem.ldb, 16)
+    sy.dma_start(U0[:, 4:68], T.u[:, :]).then_inc(sem.ldu, 16)
+    sc.dma_start(Bb[:, :], T.b[:, :]).then_inc(sem.ldb, 16)
 
-    fill(U0[:, 0:4], 0.0)
-    fill(U0[:, 68:72], 0.0)
-    fill(Bb[:, 0:4], 0.0)
-    fill(Bb[:, 68:72], 0.0)
-    fill(T.chp[:, :], 0.5)
-    fill(T.c8[:, :], 0.125)
-    fill(T1[:, :], 0.0)
+    m1 = done(v.memset(U0[:, 0:4], 0.0))
+    m2 = done(v.memset(U0[:, 68:72], 0.0))
+    m3 = done(v.memset(Z8[:, 0:2], 0.0))
+    m4 = done(v.memset(Z8[:, 66:68], 0.0))
+    m5 = done(v.memset(Big[:, 6:8], 0.0))
 
     left, right = peer(-1), peer(1)
     heng = engines([left, right])
@@ -110,79 +87,73 @@ def rank_program(g, core, T, topo):
     g.wait_ge(sem.ldu, 16)
     g.remote_dma_fused([
         RemoteDMATransfer(dst_ids=[dst_id(left)], dma_engine_mask=sum(heng[:half]), remote_sem=sem.halo,
-                          src=U0[:, 4:6], dst=T.H[:, 2:4]),
+                          src=U0[:, 4:6], dst=H[:, 2:4]),
         RemoteDMATransfer(dst_ids=[dst_id(right)], dma_engine_mask=sum(heng[half:]), remote_sem=sem.halo,
-                          src=U0[:, 66:68], dst=T.H[:, 0:2]),
+                          src=U0[:, 66:68], dst=H[:, 0:2]),
     ], local_sem=sem.sent)
 
+    sc.wait_ge(sem.ldu, 16)
+    s1 = done(sc.activation(U8[:, 0:64], U0[:, 4:68], Copy, scale=8.0))
+    sc.wait_ge(sem.ldb, 16)
+    s2 = done(sc.activation(B4[:, :], Bb[:, :], Copy, scale=4.0))
+
+    need(v, m1, m2)
     v.wait_ge(sem.ldu, 16)
-    tt(P[:, :], U0[:, 0:71], U0[:, 1:72], add, "va", A_)
-    v.wait_ge(sem.ldb, 16)
-    tt(HB[:, :], Bb[:, 2:70], T.chp[:, :], mul, "vc")
-    tt(Q[:, :], P[:, 0:68], P[:, 3:71], add, "va", A_)
-    tt(Zs[:, :], HB[:, :], U0[:, 2:70], sub, "vb", C_)
-    tt(Q8[:, :], Q[:, :], T.c8[:, :], mul, "va", A_)
-    tt(NZ[:, :], U0[:, 2:70], HB[:, :], sub, "vc")
-    tt(Big[:, 20:84], Q8[:, 0:64], Zs[:, 0:64], add, "va", ("va", "vb"))
-    tt(ND[:, :], NZ[:, 4:64], Q8[:, 4:64], sub, "vc", C_)
-    tt(Big[:, 0:4], Q8[:, 64:68], Zs[:, 64:68], add, "vb")
-    tt(DD[:, :], Big[:, 24:84], ND[:, :], mul, "va", ("va", "vc"))
-    tt(AD[:, :], Big[:, 24:84], ND[:, :], mx, "vb")
-    tt(T1[:, 0:30], DD[:, 0:30], DD[:, 30:60], add, "va", A_)
-    tt(T1[:, 32:62], AD[:, 0:30], AD[:, 30:60], mx, "vb", B_)
-    tt(T2[:, 0:16], T1[:, 0:16], T1[:, 16:32], add, "va", A_)
-    tt(T2[:, 16:32], T1[:, 32:48], T1[:, 48:64], mx, "vb", B_)
-    tt(Big[:, 12:20], T2[:, 0:8], T2[:, 8:16], add, "va", A_)
-    tt(Big[:, 4:12], T2[:, 16:24], T2[:, 24:32], mx, "vb", B_)
+    p = tt(P[:, :], U0[:, 0:71], U0[:, 1:72], add)
+    need(v, s1, s2)
+    z = tt(Z8[:, 2:66], B4[:, :], U8[:, 0:64], sub)
+    need(v, p)
+    q = tt(Q[:, 0:68], P[:, 0:68], P[:, 3:71], add)
+    need(v, m3, m4, z, q)
+    d = tt(Big[:, 8:72], Q[:, 0:64], Z8[:, 0:64], add)
+    a = tt(Big[:, 0:4], Q[:, 64:68], Z8[:, 64:68], add)
+    need(v, d)
+    mm = done(v.tensor_reduce(Big[:, 4:5], Big[:, 12:72], X, mx, apply_absolute_value=True))
+    need(sc, d)
+    s3 = done(sc.activation(T.J[:, :], Big[:, 12:72], Square, scale=kq, accum_out=Big[:, 5:6]))
 
     others = [peer(j) for j in range(1, n)]
     eng = engines(others)
-    g.wait_ge(sem.va, cnt["va"])
-    g.wait_ge(sem.vb, cnt["vb"])
+    need(g, m5, d, a, mm, s3)
     g.remote_dma_fused([
         RemoteDMATransfer(dst_ids=[dst_id(c) for c in others], dma_engine_mask=sum(eng), remote_sem=sem.arr,
-                          srcs=[Big[:, 0:24]], dsts=[F[:, n - j, :] for j in range(1, n)]),
+                          srcs=[Big[:, 0:12]], dsts=[F[:, n - j, :] for j in range(1, n)]),
     ], local_sem=sem.sent)
 
-    cp(F[:, 0, :], Big[:, 0:24], ("va", "vb"))
-    cp(F[:, n, 20:24], Big[:, 20:24])
-    tt(Ys[:, 0:62], Big[:, 22:84], U0[:, 4:66], add, "va")
-    tt(Ys[:, 62:64], Big[:, 0:2], U0[:, 66:68], add, "va")
-    fill(X1[:, :], 0.0)
-    fill(Z[:, :, :], 0.0)
-    fill(T.cf[:, :], -1.0 / ncol)
+    y8 = tt(Y8[:, :], Q[:, 2:66], B4[:, :], add)
+    c5 = done(v.tensor_copy(F[:, n, 8:12], Big[:, 8:12]))
+    need(v, m5, a, mm, s3)
+    c0 = done(v.tensor_copy(F[:, 0, :], Big[:, 0:12]))
     v.wait_ge(sem.halo, len(heng))
-    tt(H8[:, :], T.H[:, :], T.c8[:, 0:4], mul, "vc")
-    tt(Ys[:, 0:2], Ys[:, 0:2], H8[:, 0:2], add, "vc", ("va", "vc"))
-    tt(Ys[:, 62:64], Ys[:, 62:64], H8[:, 2:4], add, "vb")
-    tt(Ys[:, 0:1], Ys[:, 0:1], H8[:, 1:2], add, "yr", C_)
-    tt(Ys[:, 63:64], Ys[:, 63:64], H8[:, 2:3], add, "yr", B_)
+    h1 = tt(Hc[:, 0:2], H[:, 0:4:3], H[:, 1:3], add)
+    need(v, y8)
+    e1 = tt(Y8[:, 1:63:61], Y8[:, 1:63:61], H[:, 1:3], add)
+    need(v, h1)
+    e0 = tt(Y8[:, 0:64:63], Y8[:, 0:64:63], Hc[:, 0:2], add)
+    need(v, e0, e1)
+    ys = done(v.tensor_scalar(Ys[:, :], Y8[:, :], 0.125, None, mul))
+    need(sy, ys)
+    sy.dma_start(T.y[:, :], Ys[:, :]).then_inc(sem.sty, 16)
 
+    need(v, c0, c5)
     v.wait_ge(sem.arr, (n - 1) * len(eng))
-    tt(De[:, :, :], F[:, 0:n, 0:4], F[:, 1:n + 1, 20:24], add, "va")
-    tt(T.Sa[:, :], F[:, 0:n, 12:16], F[:, 0:n, 16:20], add, "vc")
-    tt(Dn[:, :, :], Z[:, :, :], De[:, :, :], sub, "va", A_)
-    tt(T.Ma[:, :], F[:, 0:n, 4:8], F[:, 0:n, 8:12], mx, "vc")
-    tt(T.SQ[:, :], De[:, :, :], Dn[:, :, :], mul, "va", A_)
-    tt(T.AE[:, :], De[:, :, :], Dn[:, :, :], mx, "vb")
-    tt(X1[:, 0:20], T.SQ[:, :], T.Sa[:, :], add, "va", ("va", "vc"))
-    tt(X1[:, 32:52], T.AE[:, :], T.Ma[:, :], mx, "vb", B_)
-    tt(X2[:, 0:16], X1[:, 0:16], X1[:, 16:32], add, "va", A_)
-    tt(X2[:, 16:32], X1[:, 32:48], X1[:, 48:64], mx, "vb", B_)
-    tt(X3[:, 0:8], X2[:, 0:8], X2[:, 8:16], add, "va", A_)
-    tt(X3[:, 8:16], X2[:, 16:24], X2[:, 24:32], mx, "vb", B_)
-    tt(X4[:, 0:4], X3[:, 0:4], X3[:, 4:8], add, "va", A_)
-    tt(X4[:, 4:8], X3[:, 8:12], X3[:, 12:16], mx, "vb", B_)
-    tt(X5[:, 0:2], X4[:, 0:2], X4[:, 2:4], add, "va", A_)
-    tt(X5[:, 2:4], X4[:, 4:6], X4[:, 6:8], mx, "vb", B_)
-    tt(T.rs[:, :], X5[:, 0:1], X5[:, 1:2], add, "va", A_)
-    tt(T.so[:, 1:2], X5[:, 2:3], X5[:, 3:4], mx, "sr", B_)
-    tt(T.so[:, 0:1], T.rs[:, :], T.cf[:, :], mul, "sr", A_)
+    v1 = tt(G[:, 0:20], F[:, 0:n, 0:4], F[:, 1:n + 1, 8:12], add)
+    v2 = done(v.tensor_copy(G[:, 20:25], F[:, 0:n, 4:5]))
+    v4 = done(v.tensor_copy(Hs[:, 20:25], F[:, 0:n, 5:6]))
+    need(sc, v1)
+    s4 = done(sc.activation(Hs[:, 0:20], G[:, 0:20], Square, scale=kq))
+    need(v, v1, v2)
+    v5 = done(v.tensor_reduce(T.R[:, :], G[:, 0:25], X, mx, apply_absolute_value=True))
+    need(v, v4, s4)
+    v6 = done(v.tensor_reduce(T.so[:, 0:1], Hs[:, 0:25], X, add))
+    need(v, v5)
+    v7 = done(v.tensor_scalar(T.so[:, 1:2], T.R[:, :], 0.125, None, mul))
 
-    g.scalar.wait_ge(sem.yr, 2)
-    g.scalar.dma_start(T.y[:, :], Ys[:, :]).then_inc(sem.sty, 16)
-    g.scalar.wait_ge(sem.sty, 16)
-    g.sync.wait_ge(sem.sr, 2)
-    g.sync.dma_start(T.s[:, :], T.so[:, :]).then_inc(sem.sts, 16)
-    g.sync.wait_ge(sem.sts, 16)
+    need(sy, v6, v7)
+    sy.dma_start(T.s[:, :], T.so[:, :]).then_inc(sem.sts, 16)
+    sy.wait_ge(sem.sty, 16)
+    sy.wait_ge(sem.sts, 16)
     g.wait_ge(sem.sent, len(eng) + len(heng))
+    for i in range(used[0]):
+        if "k%d" % i not in waited:
+            g.wait_ge(sem["k%d" % i], 1)

@@ -4,23 +4,23 @@ from concourse.mybir import AluOpType, AxisListType, ActivationFunctionType
 
 F32 = "float32"
 SCRATCH = {
-    "U0": ("sbuf", [128, 72], F32),
+    "Ub": ("sbuf", [128, 64], F32),
     "Bb": ("sbuf", [128, 64], F32),
-    "U8": ("psum", [128, 512], F32),
-    "B4": ("sbuf", [128, 64], F32),
-    "P": ("sbuf", [128, 71], F32),
-    "Q": ("psum", [128, 512], F32),
-    "Z8": ("sbuf", [128, 68], F32),
-    "Big": ("sbuf", [128, 72], F32),
-    "J": ("sbuf", [128, 60], F32),
-    "F": ("sbuf", [128, 6, 12], F32),
+    "W8": ("sbuf", [128, 76], F32),
+    "Un": ("psum", [128, 512], F32),
+    "HB": ("sbuf", [128, 64], F32),
+    "S5": ("psum", [128, 512], F32),
+    "Z": ("sbuf", [128, 68], F32),
+    "Big": ("sbuf", [128, 74], F32),
+    "J": ("sbuf", [128, 68], F32),
+    "F": ("sbuf", [128, 6, 16], F32),
     "G": ("sbuf", [128, 25], F32),
     "Hs": ("sbuf", [128, 25], F32),
-    "R": ("sbuf", [128, 1], F32),
     "so": ("sbuf", [128, 2], F32),
-    "Y8": ("sbuf", [128, 64], F32),
+    "Y1": ("sbuf", [128, 64], F32),
     "Ys": ("sbuf", [128, 64], F32),
     "H": ("sbuf", [128, 4], F32),
+    "H8": ("sbuf", [128, 4], F32),
     "Hc": ("sbuf", [128, 2], F32),
 }
 NK = 40
@@ -32,12 +32,12 @@ def rank_program(g, core, T, topo):
     if rank is None:
         return
     n = len(T.cores)
+    ncol = n * 64.0
     sem = T.sem
     v, sc, sy = g.vector, g.scalar, g.sync
     add, sub, mul, mx = AluOpType.add, AluOpType.subtract, AluOpType.mult, AluOpType.max
     X = AxisListType.X
     Copy, Square = ActivationFunctionType.Copy, ActivationFunctionType.Square
-    kq = 1.0 / (8.0 * math.sqrt(n * 64.0))
 
     used = [0]
     waited = {}
@@ -69,17 +69,16 @@ def rank_program(g, core, T, topo):
             m &= topo.mask(core, c)
         return [1 << i for i in range(16) if (m >> i) & 1]
 
-    U0, Bb, U8, B4, P, Q, Z8, Big, F, G, Hs, Y8, Ys, H, Hc = (T.U0, T.Bb, T.U8, T.B4, T.P, T.Q, T.Z8, T.Big, T.F, T.G,
-                                                              T.Hs, T.Y8, T.Ys, T.H, T.Hc)
+    Ub, Bb, W8, Un, HB, S5, Z, Big, F, G, Hs, Y1, Ys, H, H8, Hc = (T.Ub, T.Bb, T.W8, T.Un, T.HB, T.S5, T.Z, T.Big, T.F,
+                                                                   T.G, T.Hs, T.Y1, T.Ys, T.H, T.H8, T.Hc)
 
-    sy.dma_start(U0[:, 4:68], T.u[:, :]).then_inc(sem.ldu, 16)
+    sy.dma_start(Ub[:, :], T.u[:, :]).then_inc(sem.ldu, 16)
     sc.dma_start(Bb[:, :], T.b[:, :]).then_inc(sem.ldb, 16)
 
-    m1 = done(v.memset(U0[:, 0:4], 0.0))
-    m2 = done(v.memset(U0[:, 68:72], 0.0))
-    m3 = done(v.memset(Z8[:, 0:2], 0.0))
-    m4 = done(v.memset(Z8[:, 66:68], 0.0))
-    m5 = done(v.memset(Big[:, 6:8], 0.0))
+    m1 = done(v.memset(W8[:, 0:8], 0.0))
+    m2 = done(v.memset(W8[:, 72:76], 0.0))
+    m3 = done(v.memset(Z[:, 0:2], 0.0))
+    m4 = done(v.memset(Z[:, 66:68], 0.0))
 
     left, right = peer(-1), peer(1)
     heng = engines([left, right])
@@ -87,69 +86,71 @@ def rank_program(g, core, T, topo):
     g.wait_ge(sem.ldu, 16)
     g.remote_dma_fused([
         RemoteDMATransfer(dst_ids=[dst_id(left)], dma_engine_mask=sum(heng[:half]), remote_sem=sem.halo,
-                          src=U0[:, 4:6], dst=H[:, 2:4]),
+                          src=Ub[:, 0:2], dst=H[:, 2:4]),
         RemoteDMATransfer(dst_ids=[dst_id(right)], dma_engine_mask=sum(heng[half:]), remote_sem=sem.halo,
-                          src=U0[:, 66:68], dst=H[:, 0:2]),
+                          src=Ub[:, 62:64], dst=H[:, 0:2]),
     ], local_sem=sem.sent)
 
-    sc.wait_ge(sem.ldu, 16)
-    s1 = done(sc.activation(U8[:, 0:64], U0[:, 4:68], Copy, scale=8.0))
-    sc.wait_ge(sem.ldb, 16)
-    s2 = done(sc.activation(B4[:, :], Bb[:, :], Copy, scale=4.0))
-
-    need(v, m1, m2)
     v.wait_ge(sem.ldu, 16)
-    p = tt(P[:, :], U0[:, 0:71], U0[:, 1:72], add)
+    w = done(v.tensor_scalar(W8[:, 8:72], Ub[:, :], 0.125, None, mul))
+    sc.wait_ge(sem.ldu, 16)
+    s1 = done(sc.activation(Un[:, 0:64], Ub[:, :], Copy, scale=1.125))
+    sc.wait_ge(sem.ldb, 16)
+    s2 = done(sc.activation(HB[:, :], Bb[:, :], Copy, scale=0.5))
+
+    need(v, m1, m2, w)
+    r5 = done(v.tensor_tensor_scan(S5[:, 0:68], W8[:, 8:76], W8[:, 3:71], 0.0, add, sub))
     need(v, s1, s2)
-    z = tt(Z8[:, 2:66], B4[:, :], U8[:, 0:64], sub)
-    need(v, p)
-    q = tt(Q[:, 0:68], P[:, 0:68], P[:, 3:71], add)
-    need(v, m3, m4, z, q)
-    d = tt(Big[:, 8:72], Q[:, 0:64], Z8[:, 0:64], add)
-    a = tt(Big[:, 0:4], Q[:, 64:68], Z8[:, 64:68], add)
+    z = tt(Z[:, 2:66], HB[:, :], Un[:, 0:64], sub)
+
+    need(v, m3, m4, r5, z)
+    d = tt(Big[:, 10:74], S5[:, 0:64], Z[:, 0:64], add)
+    a = tt(Big[:, 6:10], S5[:, 64:68], Z[:, 64:68], add)
+
     need(v, d)
-    mm = done(v.tensor_reduce(Big[:, 4:5], Big[:, 12:72], X, mx, apply_absolute_value=True))
-    need(sc, d)
-    s3 = done(sc.activation(T.J[:, :], Big[:, 12:72], Square, scale=kq, accum_out=Big[:, 5:6]))
+    mm = done(v.tensor_reduce(Big[:, 0:1], Big[:, 14:74], X, mx, apply_absolute_value=True))
+    b2 = done(v.tensor_scalar(Big[:, 2:6], Big[:, 10:14], 2.0 / ncol, None, mul))
+    need(sc, d, a)
+    s3 = done(sc.activation(T.J[:, :], Big[:, 6:74], Square, scale=1.0 / math.sqrt(ncol), accum_out=Big[:, 1:2]))
 
     others = [peer(j) for j in range(1, n)]
     eng = engines(others)
-    need(g, m5, d, a, mm, s3)
+    need(g, d, a, mm, b2, s3)
     g.remote_dma_fused([
         RemoteDMATransfer(dst_ids=[dst_id(c) for c in others], dma_engine_mask=sum(eng), remote_sem=sem.arr,
-                          srcs=[Big[:, 0:12]], dsts=[F[:, n - j, :] for j in range(1, n)]),
+                          srcs=[Big[:, 0:14]], dsts=[F[:, n - j, 0:14] for j in range(1, n)]),
     ], local_sem=sem.sent)
 
-    y8 = tt(Y8[:, :], Q[:, 2:66], B4[:, :], add)
-    c5 = done(v.tensor_copy(F[:, n, 8:12], Big[:, 8:12]))
-    need(v, m5, a, mm, s3)
-    c0 = done(v.tensor_copy(F[:, 0, :], Big[:, 0:12]))
+    y1 = tt(Y1[:, :], S5[:, 2:66], W8[:, 8:72], sub)
+    need(v, a, mm, b2, s3)
+    c0 = done(v.tensor_copy(F[:, 0, 0:14], Big[:, 0:14]))
+    c5 = done(v.tensor_copy(F[:, n, 0:14], Big[:, 0:14]))
+    need(v, y1)
+    y2 = tt(Ys[:, :], Y1[:, :], HB[:, :], add)
     v.wait_ge(sem.halo, len(heng))
-    h1 = tt(Hc[:, 0:2], H[:, 0:4:3], H[:, 1:3], add)
-    need(v, y8)
-    e1 = tt(Y8[:, 1:63:61], Y8[:, 1:63:61], H[:, 1:3], add)
+    h8 = done(v.tensor_scalar(H8[:, :], H[:, :], 0.125, None, mul))
+    need(v, h8, y2)
+    h1 = tt(Hc[:, 0:2], H8[:, 0:4:3], H8[:, 1:3], add)
+    e1 = tt(Ys[:, 1:63:61], Ys[:, 1:63:61], H8[:, 1:3], add)
     need(v, h1)
-    e0 = tt(Y8[:, 0:64:63], Y8[:, 0:64:63], Hc[:, 0:2], add)
-    need(v, e0, e1)
-    ys = done(v.tensor_scalar(Ys[:, :], Y8[:, :], 0.125, None, mul))
-    need(sy, ys)
+    e0 = tt(Ys[:, 0:64:63], Ys[:, 0:64:63], Hc[:, 0:2], add)
+    need(sy, e0, e1)
     sy.dma_start(T.y[:, :], Ys[:, :]).then_inc(sem.sty, 16)
 
     need(v, c0, c5)
     v.wait_ge(sem.arr, (n - 1) * len(eng))
-    v1 = tt(G[:, 0:20], F[:, 0:n, 0:4], F[:, 1:n + 1, 8:12], add)
-    v2 = done(v.tensor_copy(G[:, 20:25], F[:, 0:n, 4:5]))
-    v4 = done(v.tensor_copy(Hs[:, 20:25], F[:, 0:n, 5:6]))
-    need(sc, v1)
-    s4 = done(sc.activation(Hs[:, 0:20], G[:, 0:20], Square, scale=kq))
-    need(v, v1, v2)
-    v5 = done(v.tensor_reduce(T.R[:, :], G[:, 0:25], X, mx, apply_absolute_value=True))
-    need(v, v4, s4)
+    v1 = tt(G[:, 0:20], F[:, 0:n, 6:10], F[:, 1:n + 1, 10:14], add)
+    v3 = tt(Hs[:, 0:20], F[:, 0:n, 6:10], F[:, 1:n + 1, 2:6], mul)
+    need(sc, c0)
+    sc.wait_ge(sem.arr, (n - 1) * len(eng))
+    c1 = done(sc.activation(G[:, 20:25], F[:, 0:n, 0], Copy))
+    c2 = done(sc.activation(Hs[:, 20:25], F[:, 0:n, 1], Copy))
+    need(v, v1, c1)
+    v5 = done(v.tensor_reduce(T.so[:, 1:2], G[:, 0:25], X, mx, apply_absolute_value=True))
+    need(v, v3, c2)
     v6 = done(v.tensor_reduce(T.so[:, 0:1], Hs[:, 0:25], X, add))
-    need(v, v5)
-    v7 = done(v.tensor_scalar(T.so[:, 1:2], T.R[:, :], 0.125, None, mul))
 
-    need(sy, v6, v7)
+    need(sy, v5, v6)
     sy.dma_start(T.s[:, :], T.so[:, :]).then_inc(sem.sts, 16)
     sy.wait_ge(sem.sty, 16)
     sy.wait_ge(sem.sts, 16)

import math
from concourse.bass import DstId, RemoteDMATransfer
from concourse.mybir import AluOpType, AxisListType, ActivationFunctionType

F32 = "float32"
SCRATCH = {
    "Ub": ("sbuf", [128, 64], F32),
    "Bb": ("sbuf", [128, 64], F32),
    "W8": ("sbuf", [128, 76], F32),
    "Un": ("psum", [128, 512], F32),
    "HB": ("sbuf", [128, 64], F32),
    "S5": ("psum", [128, 512], F32),
    "Z": ("sbuf", [128, 68], F32),
    "Big": ("sbuf", [128, 74], F32),
    "J": ("sbuf", [128, 68], F32),
    "F": ("sbuf", [128, 6, 16], F32),
    "G": ("sbuf", [128, 25], F32),
    "Hs": ("sbuf", [128, 25], F32),
    "so": ("sbuf", [128, 2], F32),
    "Y1": ("sbuf", [128, 64], F32),
    "Ys": ("sbuf", [128, 64], F32),
    "H": ("sbuf", [128, 4], F32),
    "H8": ("sbuf", [128, 4], F32),
    "Hc": ("sbuf", [128, 2], F32),
}
NK = 40
SEMAPHORES = ["ldu", "ldb", "arr", "halo", "sent", "sty", "sts"] + ["k%d" % i for i in range(NK)]


def rank_program(g, core, T, topo):
    rank = T.rank_of(core)
    if rank is None:
        return
    n = len(T.cores)
    ncol = n * 64.0
    sem = T.sem
    v, sc, sy = g.vector, g.scalar, g.sync
    add, sub, mul, mx = AluOpType.add, AluOpType.subtract, AluOpType.mult, AluOpType.max
    X = AxisListType.X
    Copy, Square = ActivationFunctionType.Copy, ActivationFunctionType.Square

    used = [0]
    waited = {}

    def done(ins):
        nm = "k%d" % used[0]
        used[0] += 1
        ins.then_inc(sem[nm], 1)
        return nm

    def need(q, *names):
        for nm in names:
            q.wait_ge(sem[nm], 1)
            waited[nm] = True

    def tt(out, a, b, op):
        return done(v.tensor_tensor(out, a, b, op))

    def peer(j):
        return T.cores[(rank + j) % n]

    def dst_id(c):
        rid, pid, _ = topo.addr(c)
        return DstId(rid=rid, pnc=pid)

    def engines(dsts):
        m = topo.mask(core, dsts[0])
        for c in dsts[1:]:
            m &= topo.mask(core, c)
        return [1 << i for i in range(16) if (m >> i) & 1]

    Ub, Bb, W8, Un, HB, S5, Z, Big, F, G, Hs, Y1, Ys, H, H8, Hc = (T.Ub, T.Bb, T.W8, T.Un, T.HB, T.S5, T.Z, T.Big, T.F,
                                                                   T.G, T.Hs, T.Y1, T.Ys, T.H, T.H8, T.Hc)

    sy.dma_start(Ub[:, :], T.u[:, :]).then_inc(sem.ldu, 16)
    sc.dma_start(Bb[:, :], T.b[:, :]).then_inc(sem.ldb, 16)

    m1 = done(v.memset(W8[:, 0:8], 0.0))
    m2 = done(v.memset(W8[:, 72:76], 0.0))
    m3 = done(v.memset(Z[:, 0:2], 0.0))
    m4 = done(v.memset(Z[:, 66:68], 0.0))

    left, right = peer(-1), peer(1)
    heng = engines([left, right])
    half = len(heng) // 2
    g.wait_ge(sem.ldu, 16)
    g.remote_dma_fused([
        RemoteDMATransfer(dst_ids=[dst_id(left)], dma_engine_mask=sum(heng[:half]), remote_sem=sem.halo,
                          src=Ub[:, 0:2], dst=H[:, 2:4]),
        RemoteDMATransfer(dst_ids=[dst_id(right)], dma_engine_mask=sum(heng[half:]), remote_sem=sem.halo,
                          src=Ub[:, 62:64], dst=H[:, 0:2]),
    ], local_sem=sem.sent)

    v.wait_ge(sem.ldu, 16)
    w = done(v.tensor_scalar(W8[:, 8:72], Ub[:, :], 0.125, None, mul))
    sc.wait_ge(sem.ldu, 16)
    s1 = done(sc.activation(Un[:, 0:64], Ub[:, :], Copy, scale=1.125))
    sc.wait_ge(sem.ldb, 16)
    s2 = done(sc.activation(HB[:, :], Bb[:, :], Copy, scale=0.5))

    need(v, m1, m2, w)
    r5 = done(v.tensor_tensor_scan(S5[:, 0:68], W8[:, 8:76], W8[:, 3:71], 0.0, add, sub))
    need(v, s1, s2)
    z = tt(Z[:, 2:66], HB[:, :], Un[:, 0:64], sub)

    need(v, m3, m4, r5, z)
    d = tt(Big[:, 10:74], S5[:, 0:64], Z[:, 0:64], add)
    a = tt(Big[:, 6:10], S5[:, 64:68], Z[:, 64:68], add)

    need(v, d)
    mm = done(v.tensor_reduce(Big[:, 0:1], Big[:, 14:74], X, mx, apply_absolute_value=True))
    b2 = done(v.tensor_scalar(Big[:, 2:6], Big[:, 10:14], 2.0 / ncol, None, mul))
    need(sc, d, a)
    s3 = done(sc.activation(T.J[:, :], Big[:, 6:74], Square, scale=1.0 / math.sqrt(ncol), accum_out=Big[:, 1:2]))

    others = [peer(j) for j in range(1, n)]
    eng = engines(others)
    need(g, d, a, mm, b2, s3)
    g.remote_dma_fused([
        RemoteDMATransfer(dst_ids=[dst_id(c) for c in others], dma_engine_mask=sum(eng), remote_sem=sem.arr,
                          srcs=[Big[:, 0:14]], dsts=[F[:, n - j, 0:14] for j in range(1, n)]),
    ], local_sem=sem.sent)

    y1 = tt(Y1[:, :], S5[:, 2:66], W8[:, 8:72], sub)
    need(v, a, mm, b2, s3)
    c0 = done(v.tensor_copy(F[:, 0, 0:14], Big[:, 0:14]))
    c5 = done(v.tensor_copy(F[:, n, 0:14], Big[:, 0:14]))
    need(v, y1)
    y2 = tt(Ys[:, :], Y1[:, :], HB[:, :], add)
    v.wait_ge(sem.halo, len(heng))
    h8 = done(v.tensor_scalar(H8[:, :], H[:, :], 0.125, None, mul))
    need(v, h8, y2)
    h1 = tt(Hc[:, 0:2], H8[:, 0:4:3], H8[:, 1:3], add)
    e1 = tt(Ys[:, 1:63:61], Ys[:, 1:63:61], H8[:, 1:3], add)
    need(v, h1)
    e0 = tt(Ys[:, 0:64:63], Ys[:, 0:64:63], Hc[:, 0:2], add)
    need(sy, e0, e1)
    sy.dma_start(T.y[:, :], Ys[:, :]).then_inc(sem.sty, 16)

    need(v, c0, c5)
    v.wait_ge(sem.arr, (n - 1) * len(eng))
    v1 = tt(G[:, 0:20], F[:, 0:n, 6:10], F[:, 1:n + 1, 10:14], add)
    v3 = tt(Hs[:, 0:20], F[:, 0:n, 6:10], F[:, 1:n + 1, 2:6], mul)
    need(sc, c0)
    sc.wait_ge(sem.arr, (n - 1) * len(eng))
    c1 = done(sc.activation(G[:, 20:25], F[:, 0:n, 0], Copy))
    c2 = done(sc.activation(Hs[:, 20:25], F[:, 0:n, 1], Copy))
    need(v, v1, c1)
    v5 = done(v.tensor_reduce(T.so[:, 1:2], G[:, 0:25], X, mx, apply_absolute_value=True))
    need(v, v3, c2)
    v6 = done(v.tensor_reduce(T.so[:, 0:1], Hs[:, 0:25], X, add))

    need(sy, v5, v6)
    sy.dma_start(T.s[:, :], T.so[:, :]).then_inc(sem.sts, 16)
    sy.wait_ge(sem.sty, 16)
    sy.wait_ge(sem.sts, 16)
    g.wait_ge(sem.sent, len(eng) + len(heng))
    for i in range(used[0]):
        if "k%d" % i not in waited:
            g.wait_ge(sem["k%d" % i], 1)
